import numpy as np
import ml_dtypes


def mxq(x, axis, fmt="e4m3"):
    dtype, down = {"e4m3": (ml_dtypes.float8_e4m3fn, 7), "e5m2": (ml_dtypes.float8_e5m2, 14)}[fmt]
    v = np.moveaxis(np.asarray(x, np.float32).astype(ml_dtypes.bfloat16).astype(np.float64), axis, -1)
    blocks = v.reshape(v.shape[:-1] + (-1, 32))
    amax = np.abs(blocks).max(-1, keepdims=True)
    byte = np.maximum(np.where(amax > 0, np.frexp(amax)[1] - 1 + 127, 0) - down, 1)
    scale = np.exp2(byte - 127.0)
    codes = (blocks / scale).astype(np.float32).astype(dtype).astype(np.float64)
    return np.moveaxis((codes * scale).reshape(v.shape), -1, axis)


WIDE = False


def mx_kscale(k, group=512):
    if not WIDE:
        return np.ones(k)
    levels = np.array([18, -18])
    if group != 512:
        return np.exp2(np.random.permutation(np.resize(levels, k // group))).repeat(group)
    if k % 512:
        return np.exp2(np.random.permutation(np.resize(levels, k // 32))).repeat(32)
    a = np.empty((k // 512, 16))
    for p in range(k // 512):
        a[p, :8] = np.random.permutation(np.resize(levels, 8))
        for g in range(8):
            far = levels[np.abs(levels - a[p, g]) >= 10]
            a[p, g + 8] = far[np.random.randint(len(far))]
    return np.exp2(a.ravel()).repeat(32)


def f64(x):
    return np.asarray(x).astype(np.float64)


G, D, M, F, O, N = 4, 128, 128, 128, 128, 512


def sgn(shape):
    return np.random.uniform(0.5, 2.0, shape) * np.where(np.random.standard_normal(shape) < 0, -1.0, 1.0)


def setup_inputs():
    n = np.random.standard_normal
    s_d = mx_kscale(D, 0)
    s_f = mx_kscale(F, 0)
    return {
        "x": (n((G, D, N)) * s_d[:, None]).astype(np.float32),
        "w": (n((G, D, M)) / np.sqrt(D) / s_d[:, None]).astype(np.float32),
        "pa": (np.random.uniform(0.05, 0.5, (G, M, 1))).astype(np.float32),
        "hs": (sgn((G, M, 1)) * np.tile(s_f.reshape(F // G, G).T, (1, G))[:, :, None]).astype(np.float32),
        "v": (n((G, F, O)) / np.sqrt(F) / s_f[:, None]).astype(np.float32),
        "cs": (np.random.uniform(0.5, 2.0, (G, O, 1))).astype(np.float32),
        "cb": (0.5 * n((G, O, 1))).astype(np.float32),
    }


def reference(x, w, pa, hs, v, cs, cb):
    wq = mxq(f64(w), 1, "e4m3")
    xq = mxq(f64(x), 1, "e4m3")
    z = wq.transpose(0, 2, 1) @ xq
    h = (np.maximum(z, 0.0) + f64(pa) * np.minimum(z, 0.0)) * f64(hs)
    u = h.reshape(G * M, N).reshape(G, M, N).transpose(1, 0, 2).reshape(G, M, N)
    vq = mxq(f64(v), 1, "e4m3")
    uq = mxq(u, 1, "e4m3")
    y = vq.transpose(0, 2, 1) @ uq
    a = y * f64(cs) + f64(cb)
    return a

@@ -1,0 +1,193 @@
+from contextlib import ExitStack
+
+import concourse.mybir as mybir
+
+G, D, N = 4, 128, 512
+FLOPS = 2 * 2 * G * D * D * N
+
+F32 = mybir.dt.float32
+BF16 = mybir.dt.bfloat16
+U32 = mybir.dt.uint32
+U8 = mybir.dt.uint8
+FP8X4 = mybir.dt.float8_e4m3fn_x4
+ALU = mybir.AluOpType
+ACT = mybir.ActivationFunctionType
+
+P = 128
+PACK = 4
+ROWS = 32
+MM_N = 128
+CHUNKS = (256, 256)
+PITCH = 8
+
+
+def walk_src(t):
+    return t.rearrange("p t (c i) -> p c t i", i=4)
+
+
+def walk_dst(t):
+    return t.rearrange("p (c i) t -> p c t i", i=4)
+
+
+def quantize(nc, operand, grouped):
+    nc.vector.quantize_mx(out=operand[0][:].bitcast(FP8X4), scales=operand[1][:], in_=grouped[:].rearrange("p n j -> p (n j)"))
+
+
+def tile_rows_monarch_prelu_kernel(tc, x, w, pa, hs, v, cs, cb, out):
+    nc = tc.nc
+    starts = [sum(CHUNKS[:c]) for c in range(len(CHUNKS))]
+    with ExitStack() as ctx:
+        sb = ctx.enter_context(tc.tile_pool(name="sb", bufs=1))
+        ps = ctx.enter_context(tc.psum_pool(name="ps", bufs=1))
+        ctx.enter_context(tc.manual_schedule())
+
+        def tile(name, shape, dtype):
+            return sb.tile(shape, dtype, name=name, align_bytes=64)
+
+        def operand(name, width):
+            return tile(name + "_codes", [P, width], U32), tile(name + "_scales", [P, width], U8)
+
+        banks = [[ps.tile([P, N], F32, name="bank%d_%d" % (s, g)) for g in range(G)] for s in range(2)]
+
+        def sums(stage, c, g):
+            return banks[c % 2][g][:, 256 * stage : 256 * stage + CHUNKS[c]]
+
+        rows = tile("rows", [P, ROWS], F32)
+        w_raw = tile("w_raw", [P, PACK, D], F32)
+        v_raw = tile("v_raw", [P, PACK, D], F32)
+        x_raw = [tile("x_raw%d" % c, [P, PACK, n], F32) for c, n in enumerate(CHUNKS)]
+        x_rows = x.rearrange("g (p j) n -> (g p) j n", j=PACK)
+        par = tile("par", [P, ROWS], F32)
+        par3 = par[:].rearrange("p (g r) -> p g r", g=G)
+        s_pa = tile("s_pa", [P, G], F32)
+        s_hs = tile("s_hs", [P, G], F32)
+        sign = tile("sign", [P, G], F32)
+        gain = tile("gain", [P, G], F32)
+        w_bf = tile("w_bf", [P, D, PACK], BF16)
+        v_bf = tile("v_bf", [P, D, PACK], BF16)
+        w_q = operand("w", D)
+        v_q = operand("v", D)
+        x_bf = [tile("x_bf%d" % c, [P, n, PACK], BF16) for c, n in enumerate(CHUNKS)]
+        x_q = [operand("x%d" % c, n) for c, n in enumerate(CHUNKS)]
+        t32 = [[tile("t%d_%d" % (c, g), [P, n], F32) for g in range(G)] for c, n in enumerate(CHUNKS)]
+        h_bf = [tile("h_bf%d" % c, [P, G, n], BF16) for c, n in enumerate(CHUNKS)]
+        u_bf = [tile("u_bf%d" % c, [P, n, G], BF16) for c, n in enumerate(CHUNKS)]
+        u_q = [operand("u%d" % c, n) for c, n in enumerate(CHUNKS)]
+        res = [[tile("res%d_%d" % (c, g), [P, n], F32) for g in range(G)] for c, n in enumerate(CHUNKS)]
+
+        def cols(c):
+            return slice(starts[c], starts[c] + CHUNKS[c])
+
+        def load_x(c):
+            nc.sync.dma_start(out=x_raw[c][:], in_=x_rows[:, :, cols(c)])
+
+        def load_weights(raw, src):
+            nc.sync.dma_start(out=raw[:], in_=src.rearrange("g (p j) m -> (g p) j m", j=PACK))
+
+        def load_vectors():
+            for r, vec in enumerate((pa, hs, cs, cb)):
+                nc.sync.dma_start(out=rows[r:P:PITCH, :], in_=vec.rearrange("g (q i) o -> q g (i o)", q=G))
+
+        def product(stage, stationary, moving, c):
+            for g in range(G):
+                part = slice(ROWS * g, ROWS * (g + 1))
+                for n0 in range(0, CHUNKS[c], MM_N):
+                    nc.tensor.matmul_mx(
+                        out=sums(stage, c, g)[:, n0 : n0 + MM_N],
+                        lhsT=stationary[0][part, :].bitcast(FP8X4),
+                        lhsT_scale=stationary[1][part, :],
+                        rhs=moving[0][part, n0 : n0 + MM_N].bitcast(FP8X4),
+                        rhs_scale=moving[1][part, n0 : n0 + MM_N],
+                        start=True,
+                        stop=True,
+                    )
+
+        def interleave_v(dst, src, a, b):
+            nc.vector.tensor_copy(out=walk_dst(dst[:, a:b, :]), in_=walk_src(src[:, :, a:b]))
+
+        def interleave_s(dst, src, a, b):
+            nc.scalar.activation(out=walk_dst(dst[:, a:b, :]), in_=walk_src(src[:, :, a:b]), func=ACT.Copy)
+
+        def interleave_sc(dst, src, a, b):
+            nc.scalar.copy(out=walk_dst(dst[:, a:b, :]), in_=walk_src(src[:, :, a:b]))
+
+        def scale_z(c, g):
+            nc.scalar.activation(out=t32[c][g][:], in_=sums(0, c, g), func=ACT.Copy, scale=gain[:, g : g + 1])
+
+        def prelu(c, g):
+            nc.vector.scalar_tensor_tensor(
+                out=h_bf[c][:, g, :], in0=t32[c][g][:], scalar=par3[:, g, 0:1], in1=t32[c][g][:], op0=ALU.mult, op1=ALU.max
+            )
+
+        def finish(c, g, on_vector):
+            factor = par3[:, g, 2:3]
+            bias = par3[:, g, 3:4]
+            if on_vector:
+                nc.vector.tensor_scalar(out=res[c][g][:], in0=sums(1, c, g), scalar1=factor, scalar2=bias, op0=ALU.mult, op1=ALU.add)
+            else:
+                nc.scalar.activation(out=res[c][g][:], in_=sums(1, c, g), func=ACT.Identity, bias=bias, scale=factor)
+            nc.sync.dma_start(out=out[g, :, cols(c)], in_=res[c][g][:])
+
+        def turn():
+            nc.vector.transpose(out=par[:], in_=rows[:])
+
+        def sides():
+            nc.vector.tensor_scalar(out=s_pa[:], in0=par3[:, :, 0], scalar1=1.0, scalar2=0.5, op0=ALU.is_le, op1=ALU.subtract)
+            nc.vector.tensor_scalar(out=s_hs[:], in0=par3[:, :, 1], scalar1=0.0, scalar2=0.5, op0=ALU.is_ge, op1=ALU.subtract)
+
+        def make_sign():
+            nc.vector.scalar_tensor_tensor(out=sign[:], in0=s_pa[:], scalar=4.0, in1=s_hs[:], op0=ALU.mult, op1=ALU.mult)
+
+        def make_gain():
+            nc.vector.tensor_tensor(out=gain[:], in0=sign[:], in1=par3[:, :, 1], op=ALU.mult)
+
+        def sign_v():
+            nc.vector.tensor_tensor(
+                out=walk_dst(v_bf[:]),
+                in0=walk_src(v_raw[:]),
+                in1=sign[:].unsqueeze(1).unsqueeze(3).to_broadcast([P, D // 4, PACK, 4]),
+                op=ALU.mult,
+            )
+
+        nc.vector.memset(rows[:], 0.0)
+        load_x(0)
+        load_vectors()
+        load_weights(w_raw, w)
+        load_x(1)
+        load_weights(v_raw, v)
+        interleave_s(x_bf[0], x_raw[0], 176, 256)
+        interleave_v(x_bf[0], x_raw[0], 0, 176)
+        turn()
+        interleave_s(w_bf, w_raw, 0, D)
+        quantize(nc, x_q[0], x_bf[0])
+        sides()
+        quantize(nc, w_q, w_bf)
+        make_sign()
+        product(0, w_q, x_q[0], 0)
+        interleave_s(x_bf[1], x_raw[1], 160, 256)
+        interleave_v(x_bf[1], x_raw[1], 0, 160)
+        make_gain()
+        for g in range(G):
+            scale_z(0, g)
+        quantize(nc, x_q[1], x_bf[1])
+        product(0, w_q, x_q[1], 1)
+        sign_v()
+        for g in range(G):
+            scale_z(1, g)
+        prelu(0, 0)
+        quantize(nc, v_q, v_bf)
+        for g in range(1, G):
+            prelu(0, g)
+        interleave_v(u_bf[0], h_bf[0], 0, 256)
+        prelu(1, 0)
+        quantize(nc, u_q[0], u_bf[0])
+        product(1, v_q, u_q[0], 0)
+        for g in range(G):
+            finish(0, g, False)
+        for g in range(1, G):
+            prelu(1, g)
+        interleave_v(u_bf[1], h_bf[1], 0, 256)
+        quantize(nc, u_q[1], u_bf[1])
+        product(1, v_q, u_q[1], 1)
+        for g in range(G):
+            finish(1, g, g % 2 == 1)

@@ -17,7 +17,7 @@ P = 128
 PACK = 4
 ROWS = 32
 MM_N = 128
-CHUNKS = (256, 256)
+CHUNKS = (256, 128, 128)
 PITCH = 8
 
 
@@ -50,7 +50,8 @@ def tile_rows_monarch_prelu_kernel(tc, x, w, pa, hs, v, cs, cb, out):
         banks = [[ps.tile([P, N], F32, name="bank%d_%d" % (s, g)) for g in range(G)] for s in range(2)]
 
         def sums(stage, c, g):
-            return banks[c % 2][g][:, 256 * stage : 256 * stage + CHUNKS[c]]
+            place = ((0, 0), (1, 0), (1, 128)) if stage == 0 else ((0, 256), (1, 256), (0, 0))
+            return banks[place[c][0]][g][:, place[c][1] : place[c][1] + CHUNKS[c]]
 
         rows = tile("rows", [P, ROWS], F32)
         w_raw = tile("w_raw", [P, PACK, D], F32)
@@ -155,39 +156,58 @@ def tile_rows_monarch_prelu_kernel(tc, x, w, pa, hs, v, cs, cb, out):
         load_weights(w_raw, w)
         load_x(1)
         load_weights(v_raw, v)
-        interleave_s(x_bf[0], x_raw[0], 176, 256)
-        interleave_v(x_bf[0], x_raw[0], 0, 176)
+        load_x(2)
+        interleave_s(x_bf[0], x_raw[0], 160, 256)
         turn()
-        interleave_s(w_bf, w_raw, 0, D)
-        quantize(nc, x_q[0], x_bf[0])
+        interleave_v(x_bf[0], x_raw[0], 0, 160)
         sides()
+        interleave_s(w_bf, w_raw, 64, D)
+        interleave_v(w_bf, w_raw, 0, 64)
+        quantize(nc, x_q[0], x_bf[0])
         quantize(nc, w_q, w_bf)
-        make_sign()
         product(0, w_q, x_q[0], 0)
-        interleave_s(x_bf[1], x_raw[1], 160, 256)
-        interleave_v(x_bf[1], x_raw[1], 0, 160)
+        make_sign()
+        interleave_s(x_bf[1], x_raw[1], 64, 128)
+        interleave_v(x_bf[1], x_raw[1], 0, 64)
         make_gain()
         for g in range(G):
             scale_z(0, g)
         quantize(nc, x_q[1], x_bf[1])
         product(0, w_q, x_q[1], 1)
         sign_v()
+        interleave_s(x_bf[2], x_raw[2], 64, 128)
         for g in range(G):
             scale_z(1, g)
-        prelu(0, 0)
-        quantize(nc, v_q, v_bf)
-        for g in range(1, G):
+        interleave_v(x_bf[2], x_raw[2], 0, 64)
+        for g in range(G):
             prelu(0, g)
-        interleave_v(u_bf[0], h_bf[0], 0, 256)
-        prelu(1, 0)
+        quantize(nc, v_q, v_bf)
+        quantize(nc, x_q[2], x_bf[2])
+        product(0, w_q, x_q[2], 2)
+        interleave_sc(u_bf[0], h_bf[0], 160, 256)
+        interleave_v(u_bf[0], h_bf[0], 0, 160)
+        for g in range(G):
+            scale_z(2, g)
+        for g in range(2):
+            prelu(1, g)
         quantize(nc, u_q[0], u_bf[0])
         product(1, v_q, u_q[0], 0)
+        for g in range(2, G):
+            prelu(1, g)
+        for g in range(2):
+            prelu(2, g)
+        interleave_sc(u_bf[1], h_bf[1], 64, 128)
+        interleave_v(u_bf[1], h_bf[1], 0, 64)
         for g in range(G):
             finish(0, g, False)
-        for g in range(1, G):
-            prelu(1, g)
-        interleave_v(u_bf[1], h_bf[1], 0, 256)
+        for g in range(2, 4):
+            prelu(2, g)
         quantize(nc, u_q[1], u_bf[1])
         product(1, v_q, u_q[1], 1)
+        interleave_v(u_bf[2], h_bf[2], 0, 128)
+        quantize(nc, u_q[2], u_bf[2])
+        product(1, v_q, u_q[2], 2)
+        for g in range(0, G):
+            finish(1, g, False)
         for g in range(G):
-            finish(1, g, g % 2 == 1)
+            finish(2, g, g % 2 == 0)

@@ -22,11 +22,11 @@ PITCH = 8
 
 
 def walk_src(t):
-    return t.rearrange("p t (c i) -> p c t i", i=4)
+    return t.rearrange("p t (c i) -> p c t i", i=2 if t.dtype == F32 else 4)
 
 
-def walk_dst(t):
-    return t.rearrange("p (c i) t -> p c t i", i=4)
+def walk_dst(t, src):
+    return t.rearrange("p (c i) t -> p c t i", i=2 if src.dtype == F32 else 4)
 
 
 def quantize(nc, operand, grouped):
@@ -74,7 +74,7 @@ def tile_rows_monarch_prelu_kernel(tc, x, w, pa, hs, v, cs, cb, out):
         h_bf = [tile("h_bf%d" % c, [P, G, n], BF16) for c, n in enumerate(CHUNKS)]
         u_bf = [tile("u_bf%d" % c, [P, n, G], BF16) for c, n in enumerate(CHUNKS)]
         u_q = [operand("u%d" % c, n) for c, n in enumerate(CHUNKS)]
-        res = [[tile("res%d_%d" % (c, g), [P, n], F32) for g in range(G)] for c, n in enumerate(CHUNKS)]
+        res = [tile("res%d" % c, [P, G, n], F32) for c, n in enumerate(CHUNKS)]
 
         def cols(c):
             return slice(starts[c], starts[c] + CHUNKS[c])
@@ -104,13 +104,13 @@ def tile_rows_monarch_prelu_kernel(tc, x, w, pa, hs, v, cs, cb, out):
                     )
 
         def interleave_v(dst, src, a, b):
-            nc.vector.tensor_copy(out=walk_dst(dst[:, a:b, :]), in_=walk_src(src[:, :, a:b]))
+            nc.vector.tensor_copy(out=walk_dst(dst[:, a:b, :], src), in_=walk_src(src[:, :, a:b]))
 
         def interleave_s(dst, src, a, b):
-            nc.scalar.activation(out=walk_dst(dst[:, a:b, :]), in_=walk_src(src[:, :, a:b]), func=ACT.Copy)
+            nc.scalar.activation(out=walk_dst(dst[:, a:b, :], src), in_=walk_src(src[:, :, a:b]), func=ACT.Copy)
 
         def interleave_sc(dst, src, a, b):
-            nc.scalar.copy(out=walk_dst(dst[:, a:b, :]), in_=walk_src(src[:, :, a:b]))
+            nc.scalar.copy(out=walk_dst(dst[:, a:b, :], src), in_=walk_src(src[:, :, a:b]))
 
         def scale_z(c, g):
             nc.scalar.activation(out=t32[c][g][:], in_=sums(0, c, g), func=ACT.Copy, scale=gain[:, g : g + 1])
@@ -124,10 +124,12 @@ def tile_rows_monarch_prelu_kernel(tc, x, w, pa, hs, v, cs, cb, out):
             factor = par3[:, g, 2:3]
             bias = par3[:, g, 3:4]
             if on_vector:
-                nc.vector.tensor_scalar(out=res[c][g][:], in0=sums(1, c, g), scalar1=factor, scalar2=bias, op0=ALU.mult, op1=ALU.add)
+                nc.vector.tensor_scalar(out=res[c][:, g, :], in0=sums(1, c, g), scalar1=factor, scalar2=bias, op0=ALU.mult, op1=ALU.add)
             else:
-                nc.scalar.activation(out=res[c][g][:], in_=sums(1, c, g), func=ACT.Identity, bias=bias, scale=factor)
-            nc.sync.dma_start(out=out[g, :, cols(c)], in_=res[c][g][:])
+                nc.scalar.activation(out=res[c][:, g, :], in_=sums(1, c, g), func=ACT.Identity, bias=bias, scale=factor)
+
+        def store(c, g0, g1):
+            nc.sync.dma_start(out=out[g0:g1, :, cols(c)].rearrange("g o n -> o g n"), in_=res[c][:, g0:g1, :])
 
         def turn():
             nc.vector.transpose(out=par[:], in_=rows[:])
@@ -144,9 +146,9 @@ def tile_rows_monarch_prelu_kernel(tc, x, w, pa, hs, v, cs, cb, out):
 
         def sign_v():
             nc.vector.tensor_tensor(
-                out=walk_dst(v_bf[:]),
+                out=walk_dst(v_bf[:], v_raw),
                 in0=walk_src(v_raw[:]),
-                in1=sign[:].unsqueeze(1).unsqueeze(3).to_broadcast([P, D // 4, PACK, 4]),
+                in1=sign[:].unsqueeze(1).unsqueeze(3).to_broadcast([P, D // 2, PACK, 2]),
                 op=ALU.mult,
             )
 
@@ -200,6 +202,7 @@ def tile_rows_monarch_prelu_kernel(tc, x, w, pa, hs, v, cs, cb, out):
         interleave_v(u_bf[1], h_bf[1], 0, 64)
         for g in range(G):
             finish(0, g, False)
+            store(0, g, g + 1)
         for g in range(2, 4):
             prelu(2, g)
         quantize(nc, u_q[1], u_bf[1])
@@ -207,7 +210,15 @@ def tile_rows_monarch_prelu_kernel(tc, x, w, pa, hs, v, cs, cb, out):
         interleave_v(u_bf[2], h_bf[2], 0, 128)
         quantize(nc, u_q[2], u_bf[2])
         product(1, v_q, u_q[2], 2)
-        for g in range(0, G):
-            finish(1, g, False)
-        for g in range(G):
+        for g in range(2):
+            finish(1, g, g % 2 == 0)
+        store(1, 0, 2)
+        for g in range(2, G):
+            finish(1, g, g % 2 == 0)
+        store(1, 2, 4)
+        for g in range(2):
             finish(2, g, g % 2 == 0)
+        store(2, 0, 2)
+        for g in range(2, G):
+            finish(2, g, g % 2 == 0)
+        store(2, 2, 4)

from contextlib import ExitStack

import concourse.mybir as mybir

G, D, N = 4, 128, 512
FLOPS = 2 * 2 * G * D * D * N

F32 = mybir.dt.float32
BF16 = mybir.dt.bfloat16
U32 = mybir.dt.uint32
U8 = mybir.dt.uint8
FP8X4 = mybir.dt.float8_e4m3fn_x4
ALU = mybir.AluOpType
ACT = mybir.ActivationFunctionType

P = 128
PACK = 4
ROWS = 32
MM_N = 128
CHUNKS = (256, 128, 128)
PITCH = 8


def walk_src(t):
    return t.rearrange("p t (c i) -> p c t i", i=2 if t.dtype == F32 else 4)


def walk_dst(t, src):
    return t.rearrange("p (c i) t -> p c t i", i=2 if src.dtype == F32 else 4)


def quantize(nc, operand, grouped):
    nc.vector.quantize_mx(out=operand[0][:].bitcast(FP8X4), scales=operand[1][:], in_=grouped[:].rearrange("p n j -> p (n j)"))


def tile_rows_monarch_prelu_kernel(tc, x, w, pa, hs, v, cs, cb, out):
    nc = tc.nc
    starts = [sum(CHUNKS[:c]) for c in range(len(CHUNKS))]
    with ExitStack() as ctx:
        sb = ctx.enter_context(tc.tile_pool(name="sb", bufs=1))
        ps = ctx.enter_context(tc.psum_pool(name="ps", bufs=1))
        ctx.enter_context(tc.manual_schedule())

        def tile(name, shape, dtype):
            return sb.tile(shape, dtype, name=name, align_bytes=64)

        def operand(name, width):
            return tile(name + "_codes", [P, width], U32), tile(name + "_scales", [P, width], U8)

        banks = [[ps.tile([P, N], F32, name="bank%d_%d" % (s, g)) for g in range(G)] for s in range(2)]

        def sums(stage, c, g):
            place = ((0, 0), (1, 0), (1, 128)) if stage == 0 else ((0, 256), (1, 256), (0, 0))
            return banks[place[c][0]][g][:, place[c][1] : place[c][1] + CHUNKS[c]]

        rows = tile("rows", [P, ROWS], F32)
        w_raw = tile("w_raw", [P, PACK, D], F32)
        v_raw = tile("v_raw", [P, PACK, D], F32)
        x_raw = [tile("x_raw%d" % c, [P, PACK, n], F32) for c, n in enumerate(CHUNKS)]
        x_rows = x.rearrange("g (p j) n -> (g p) j n", j=PACK)
        par = tile("par", [P, ROWS], F32)
        par3 = par[:].rearrange("p (g r) -> p g r", g=G)
        s_pa = tile("s_pa", [P, G], F32)
        s_hs = tile("s_hs", [P, G], F32)
        sign = tile("sign", [P, G], F32)
        gain = tile("gain", [P, G], F32)
        w_bf = tile("w_bf", [P, D, PACK], BF16)
        v_bf = tile("v_bf", [P, D, PACK], BF16)
        w_q = operand("w", D)
        v_q = operand("v", D)
        x_bf = [tile("x_bf%d" % c, [P, n, PACK], BF16) for c, n in enumerate(CHUNKS)]
        x_q = [operand("x%d" % c, n) for c, n in enumerate(CHUNKS)]
        t32 = [[tile("t%d_%d" % (c, g), [P, n], F32) for g in range(G)] for c, n in enumerate(CHUNKS)]
        h_bf = [tile("h_bf%d" % c, [P, G, n], BF16) for c, n in enumerate(CHUNKS)]
        u_bf = [tile("u_bf%d" % c, [P, n, G], BF16) for c, n in enumerate(CHUNKS)]
        u_q = [operand("u%d" % c, n) for c, n in enumerate(CHUNKS)]
        res = [tile("res%d" % c, [P, G, n], F32) for c, n in enumerate(CHUNKS)]

        def cols(c):
            return slice(starts[c], starts[c] + CHUNKS[c])

        def load_x(c):
            nc.sync.dma_start(out=x_raw[c][:], in_=x_rows[:, :, cols(c)])

        def load_weights(raw, src):
            nc.sync.dma_start(out=raw[:], in_=src.rearrange("g (p j) m -> (g p) j m", j=PACK))

        def load_vectors():
            for r, vec in enumerate((pa, hs, cs, cb)):
                nc.sync.dma_start(out=rows[r:P:PITCH, :], in_=vec.rearrange("g (q i) o -> q g (i o)", q=G))

        def product(stage, stationary, moving, c):
            for g in range(G):
                part = slice(ROWS * g, ROWS * (g + 1))
                for n0 in range(0, CHUNKS[c], MM_N):
                    nc.tensor.matmul_mx(
                        out=sums(stage, c, g)[:, n0 : n0 + MM_N],
                        lhsT=stationary[0][part, :].bitcast(FP8X4),
                        lhsT_scale=stationary[1][part, :],
                        rhs=moving[0][part, n0 : n0 + MM_N].bitcast(FP8X4),
                        rhs_scale=moving[1][part, n0 : n0 + MM_N],
                        start=True,
                        stop=True,
                    )

        def interleave_v(dst, src, a, b):
            nc.vector.tensor_copy(out=walk_dst(dst[:, a:b, :], src), in_=walk_src(src[:, :, a:b]))

        def interleave_s(dst, src, a, b):
            nc.scalar.activation(out=walk_dst(dst[:, a:b, :], src), in_=walk_src(src[:, :, a:b]), func=ACT.Copy)

        def interleave_sc(dst, src, a, b):
            nc.scalar.copy(out=walk_dst(dst[:, a:b, :], src), in_=walk_src(src[:, :, a:b]))

        def scale_z(c, g):
            nc.scalar.activation(out=t32[c][g][:], in_=sums(0, c, g), func=ACT.Copy, scale=gain[:, g : g + 1])

        def prelu(c, g):
            nc.vector.scalar_tensor_tensor(
                out=h_bf[c][:, g, :], in0=t32[c][g][:], scalar=par3[:, g, 0:1], in1=t32[c][g][:], op0=ALU.mult, op1=ALU.max
            )

        def finish(c, g, on_vector):
            factor = par3[:, g, 2:3]
            bias = par3[:, g, 3:4]
            if on_vector:
                nc.vector.tensor_scalar(out=res[c][:, g, :], in0=sums(1, c, g), scalar1=factor, scalar2=bias, op0=ALU.mult, op1=ALU.add)
            else:
                nc.scalar.activation(out=res[c][:, g, :], in_=sums(1, c, g), func=ACT.Identity, bias=bias, scale=factor)

        def store(c, g0, g1):
            nc.sync.dma_start(out=out[g0:g1, :, cols(c)].rearrange("g o n -> o g n"), in_=res[c][:, g0:g1, :])

        def turn():
            nc.vector.transpose(out=par[:], in_=rows[:])

        def sides():
            nc.vector.tensor_scalar(out=s_pa[:], in0=par3[:, :, 0], scalar1=1.0, scalar2=0.5, op0=ALU.is_le, op1=ALU.subtract)
            nc.vector.tensor_scalar(out=s_hs[:], in0=par3[:, :, 1], scalar1=0.0, scalar2=0.5, op0=ALU.is_ge, op1=ALU.subtract)

        def make_sign():
            nc.vector.scalar_tensor_tensor(out=sign[:], in0=s_pa[:], scalar=4.0, in1=s_hs[:], op0=ALU.mult, op1=ALU.mult)

        def make_gain():
            nc.vector.tensor_tensor(out=gain[:], in0=sign[:], in1=par3[:, :, 1], op=ALU.mult)

        def sign_v():
            nc.vector.tensor_tensor(
                out=walk_dst(v_bf[:], v_raw),
                in0=walk_src(v_raw[:]),
                in1=sign[:].unsqueeze(1).unsqueeze(3).to_broadcast([P, D // 2, PACK, 2]),
                op=ALU.mult,
            )

        nc.vector.memset(rows[:], 0.0)
        load_x(0)
        load_vectors()
        load_weights(w_raw, w)
        load_x(1)
        load_weights(v_raw, v)
        load_x(2)
        interleave_s(x_bf[0], x_raw[0], 160, 256)
        turn()
        interleave_v(x_bf[0], x_raw[0], 0, 160)
        sides()
        interleave_s(w_bf, w_raw, 64, D)
        interleave_v(w_bf, w_raw, 0, 64)
        quantize(nc, x_q[0], x_bf[0])
        quantize(nc, w_q, w_bf)
        product(0, w_q, x_q[0], 0)
        make_sign()
        interleave_s(x_bf[1], x_raw[1], 64, 128)
        interleave_v(x_bf[1], x_raw[1], 0, 64)
        make_gain()
        for g in range(G):
            scale_z(0, g)
        quantize(nc, x_q[1], x_bf[1])
        product(0, w_q, x_q[1], 1)
        sign_v()
        interleave_s(x_bf[2], x_raw[2], 64, 128)
        for g in range(G):
            scale_z(1, g)
        interleave_v(x_bf[2], x_raw[2], 0, 64)
        for g in range(G):
            prelu(0, g)
        quantize(nc, v_q, v_bf)
        quantize(nc, x_q[2], x_bf[2])
        product(0, w_q, x_q[2], 2)
        interleave_sc(u_bf[0], h_bf[0], 160, 256)
        interleave_v(u_bf[0], h_bf[0], 0, 160)
        for g in range(G):
            scale_z(2, g)
        for g in range(2):
            prelu(1, g)
        quantize(nc, u_q[0], u_bf[0])
        product(1, v_q, u_q[0], 0)
        for g in range(2, G):
            prelu(1, g)
        for g in range(2):
            prelu(2, g)
        interleave_sc(u_bf[1], h_bf[1], 64, 128)
        interleave_v(u_bf[1], h_bf[1], 0, 64)
        for g in range(G):
            finish(0, g, False)
            store(0, g, g + 1)
        for g in range(2, 4):
            prelu(2, g)
        quantize(nc, u_q[1], u_bf[1])
        product(1, v_q, u_q[1], 1)
        interleave_v(u_bf[2], h_bf[2], 0, 128)
        quantize(nc, u_q[2], u_bf[2])
        product(1, v_q, u_q[2], 2)
        for g in range(2):
            finish(1, g, g % 2 == 0)
        store(1, 0, 2)
        for g in range(2, G):
            finish(1, g, g % 2 == 0)
        store(1, 2, 4)
        for g in range(2):
            finish(2, g, g % 2 == 0)
        store(2, 0, 2)
        for g in range(2, G):
            finish(2, g, g % 2 == 0)
        store(2, 2, 4)
